import numpy as np
import ml_dtypes


def mxq(x, axis, fmt="e4m3"):
    dtype, down = {"e4m3": (ml_dtypes.float8_e4m3fn, 7), "e5m2": (ml_dtypes.float8_e5m2, 14)}[fmt]
    v = np.moveaxis(np.asarray(x, np.float32).astype(ml_dtypes.bfloat16).astype(np.float64), axis, -1)
    blocks = v.reshape(v.shape[:-1] + (-1, 32))
    amax = np.abs(blocks).max(-1, keepdims=True)
    byte = np.maximum(np.where(amax > 0, np.frexp(amax)[1] - 1 + 127, 0) - down, 1)
    scale = np.exp2(byte - 127.0)
    codes = (blocks / scale).astype(np.float32).astype(dtype).astype(np.float64)
    return np.moveaxis((codes * scale).reshape(v.shape), -1, axis)


WIDE = False


def mx_kscale(k):
    if not WIDE:
        return np.ones(k)
    levels = np.array([10, -10, 5, -5, 0])
    if k % 512:
        return np.exp2(np.random.permutation(np.resize(levels, k // 32))).repeat(32)
    a = np.empty((k // 512, 16))
    for p in range(k // 512):
        a[p, :8] = np.random.permutation(np.resize(levels, 8))
        for g in range(8):
            far = levels[np.abs(levels - a[p, g]) >= 10]
            a[p, g + 8] = far[np.random.randint(len(far))]
    return np.exp2(a.ravel()).repeat(32)


def f64(x):
    return np.asarray(x).astype(np.float64)


def striped(idx):
    return np.tile(idx.reshape(-1, 16).T, (8, 1)).astype(np.uint16)


def unstriped(offs):
    return offs[:16].T.reshape(-1).astype(np.int64)


def striped8(idx):
    return np.concatenate([x.reshape(-1, 16).T for x in idx]).astype(np.uint16)


def runs(offs, k):
    lists = np.stack([offs[16 * r : 16 * r + 16].T.reshape(-1) for r in range(8)]).astype(np.int64)
    return lists[np.arange(k) % 512 // 64]


def pack_weight(w):
    k, n = w.shape
    w = f64(np.asarray(w, np.float32).astype(ml_dtypes.bfloat16)).reshape(k // 32, 32, n)
    amax = np.abs(w).max(1)
    byte = np.clip(np.where(amax > 0, np.frexp(amax)[1] - 1 + 127 - 7, 1), 1, 254)
    scaled = (w * np.exp2(127.0 - byte)[:, None, :]).reshape(k, n).astype(np.float32)
    words = np.ascontiguousarray(scaled.reshape(k // 512, 128, 4, n).transpose(0, 1, 3, 2)).astype(ml_dtypes.float8_e4m3fn).view(np.uint8)
    return words, np.ascontiguousarray(byte.astype(np.uint8).reshape(k // 512, 16, n))


def unpack_weight(words, scales):
    g, p, n, _ = words.shape
    vals = np.ascontiguousarray(words).view(ml_dtypes.float8_e4m3fn).astype(np.float64) * np.repeat(np.exp2(scales.astype(np.float64) - 127.0), 8, axis=1)[..., None]
    return vals.transpose(0, 1, 3, 2).reshape(g * 512, n)


def sigmoid(v):
    return 1.0 / (1.0 + np.exp(-np.maximum(v, -700.0)))


K, T, S, V, H = 512, 2048, 512, 512, 512


def setup_inputs():
    n = np.random.standard_normal
    s = mx_kscale(K)[:, None]
    u = mx_kscale(S)
    packed_xT = pack_weight(n((K, T)) * s)
    return {
        "x_words": packed_xT[0],
        "x_scales": packed_xT[1],
        "w1": (n((K, H)) / np.sqrt(K) / s).astype(np.float32),
        "w2": (n((K, H)) / np.sqrt(K) / s).astype(np.float32),
        "ga": (np.random.uniform(0.5, 1.5, (H, 1)) * u[:, None]).astype(np.float32),
        "gb": (np.random.uniform(0.5, 1.5, (H, 1)) / u[:, None]).astype(np.float32),
        "offs": striped(np.random.permutation(T)[:S]),
        "two": striped(np.random.permutation(T)[:V]),
        "n1": striped8(np.stack([np.random.permutation(S) for _ in range(8)])),
        "n2": striped8(np.stack([np.random.permutation(S) for _ in range(8)])),
        "n3": striped8(np.stack([np.random.permutation(V) for _ in range(8)])),
        "n4": striped8(np.stack([np.random.permutation(V) for _ in range(8)])),
        "n5": striped8(np.stack([np.random.permutation(V) for _ in range(8)])),
    }


def reference(x_words, x_scales, w1, w2, ga, gb, offs, two, n1, n2, n3, n4, n5):
    xq = unpack_weight(x_words, x_scales)[:, unstriped(offs)]
    a = mxq(f64(w1), 0, "e4m3").T @ xq
    z = f64(ga) * ((a[np.arange(H)[:, None], runs(n1, H)]) / (np.abs(a) + np.abs(a[np.arange(H)[:, None], runs(n2, H)]) + 0.5))
    x_two = unpack_weight(x_words, x_scales)[:, unstriped(two)]
    b = mxq(f64(w2), 0, "e4m3").T @ x_two
    z2 = f64(gb) * (b * (sigmoid(b[np.arange(H)[:, None], runs(n3, H)])))
    s = 0.0625 * ((mxq(z, 0, "e4m3").T @ mxq(z2, 0, "e4m3")))
    st = s + s[np.arange(S)[:, None], runs(n4, S)]
    return st * (np.tanh(st[np.arange(S)[:, None], runs(n5, S)]))

@@ -1,0 +1,206 @@
+from contextlib import ExitStack
+
+import concourse.mybir as mybir
+
+F32 = mybir.dt.float32
+BF16 = mybir.dt.bfloat16
+I32 = mybir.dt.int32
+U32 = mybir.dt.uint32
+U16 = mybir.dt.uint16
+U8 = mybir.dt.uint8
+FP8X4 = mybir.dt.float8_e4m3fn_x4
+ACT = mybir.ActivationFunctionType
+ALU = mybir.AluOpType
+
+P = 128
+PACK = 4
+T = 2048
+N = 512
+FLOPS = 3 * 2 * 512 * 512 * 512
+
+
+def tile_picked_kqnorm2gatehopp_none_p_kernel(
+    tc, x_words, x_scales, w1, w2, ga, gb, offs, two, n1, n2, n3, n4, n5, out
+):
+    nc = tc.nc
+    with ExitStack() as ctx:
+        lists = ctx.enter_context(tc.tile_pool(name="lists", bufs=1))
+        keep = ctx.enter_context(tc.tile_pool(name="keep", bufs=1))
+        psum = ctx.enter_context(tc.psum_pool(name="psum", bufs=1))
+
+        def load_list(src, name):
+            tile = lists.tile([P, N // 16], U16, name=name)
+            nc.sync.dma_start(tile[:], src)
+            return tile
+
+        warm = keep.tile([P, 2], F32, name="warm")
+        nc.vector.memset(warm[:, 0:1], 1.0)
+        nc.scalar.activation(warm[:, 1:2], warm[:, 0:1], ACT.Ln)
+
+        scale_table = keep.tile([P, T], U8, name="scale_table", align_bytes=64)
+        nc.vector.memset(scale_table[:].bitcast(I32), 0)
+
+        half = N // 2
+        word_table = keep.tile([P, T], U32, name="word_table", align_bytes=64)
+        nc.sync.dma_start(word_table[:].bitcast(I32), x_words[0].rearrange("p n t -> p (n t)").bitcast(I32))
+        for q in range(4):
+            nc.sync.dma_start(
+                scale_table[32 * q : 32 * q + 4, :].bitcast(I32),
+                x_scales[0, 4 * q : 4 * q + 4, :].bitcast(I32),
+            )
+        offs_t = load_list(offs, "offs_t")
+        two_t = load_list(two, "two_t")
+        w1_raw = [keep.tile([P, PACK, half], F32, name="w1_raw%d" % h) for h in range(2)]
+        w1_rows = w1.rearrange("(p j) c -> p j c", j=PACK)
+        for h in range(2):
+            nc.sync.dma_start(w1_raw[h][:], w1_rows[:, :, h * half : (h + 1) * half])
+        n2_t = load_list(n2, "n2_t")
+        ga_t = keep.tile([P, PACK], F32, name="ga_t")
+        nc.sync.dma_start(ga_t[:], ga.rearrange("(p t) o -> p (t o)", t=PACK))
+        n1_t = load_list(n1, "n1_t")
+        w2_raw = keep.tile([P, PACK, N], F32, name="w2_raw")
+        nc.sync.dma_start(w2_raw[:], w2.rearrange("(p j) c -> p j c", j=PACK))
+        n3_t = load_list(n3, "n3_t")
+        gb_t = keep.tile([P, PACK], F32, name="gb_t")
+        nc.sync.dma_start(gb_t[:], gb.rearrange("(p t) o -> p (t o)", t=PACK))
+        n4_t = load_list(n4, "n4_t")
+        n5_t = load_list(n5, "n5_t")
+
+        win_abs = [keep.tile([P, 2 * N], F32, name="win_abs%d" % t) for t in range(PACK)]
+        win_a = [keep.tile([P, 2 * N], F32, name="win_a%d" % t) for t in range(PACK)]
+        win_b = [keep.tile([P, 2 * N], F32, name="win_b%d" % t) for t in range(PACK)]
+        for t in range(PACK):
+            nc.vector.memset(win_abs[t][:, N:], 0.0)
+
+        def mx_tiles(name):
+            codes = keep.tile([P, N], U32, name=name + "_codes", align_bytes=64)
+            scales = keep.tile([P, N], U8, name=name + "_scales", align_bytes=64)
+            return codes, scales
+
+        def quantize(dst, grouped, cols):
+            nc.vector.quantize_mx(
+                out=dst[0][:, cols].bitcast(FP8X4),
+                scales=dst[1][:, cols],
+                in_=grouped[:, PACK * cols.start : PACK * cols.stop],
+            )
+
+        def product(bank, lhs, t, rhs, cols):
+            rows = slice(t * P, (t + 1) * P)
+            nc.tensor.matmul_mx(
+                out=bank[:, cols],
+                lhsT=lhs[0][:, rows].bitcast(FP8X4),
+                lhsT_scale=lhs[1][:, rows],
+                rhs=rhs[0][:, cols].bitcast(FP8X4),
+                rhs_scale=rhs[1][:, cols],
+                start=True,
+                stop=True,
+            )
+
+        whole = slice(0, N)
+        halves = [slice(0, half), slice(half, N)]
+        xa = mx_tiles("xa")
+        xb = mx_tiles("xb")
+        w1q = mx_tiles("w1q")
+        w2q = mx_tiles("w2q")
+        nc.vector.tensor_copy(xa[0][:], word_table[:].indirect(offs_t[:]))
+        nc.vector.tensor_copy(xb[0][:], word_table[:].indirect(two_t[:]))
+        nc.vector.tensor_copy(xa[1][:], scale_table[:].indirect(offs_t[:]))
+
+        w1_grouped = keep.tile([P, PACK * N], BF16, name="w1_grouped", align_bytes=64)
+        w1_view = w1_grouped[:].rearrange("p (t m j) -> p m j t", t=PACK, j=PACK)
+        for h in range(2):
+            nc.scalar.copy(
+                w1_view[:, h * (P // 2) : (h + 1) * (P // 2), :, :],
+                w1_raw[h][:].rearrange("p j (m t) -> p m j t", t=PACK),
+            )
+        banks_a = [psum.tile([P, N], F32, name="bank_a%d" % t, tag="first%d" % t) for t in range(PACK)]
+        banks_b = [psum.tile([P, N], F32, name="bank_b%d" % t) for t in range(PACK)]
+        for pair in halves:
+            quantize(w1q, w1_grouped, pair)
+        for t in range(PACK):
+            product(banks_a[t], w1q, t, xa, whole)
+        nc.vector.tensor_copy(xb[1][:], scale_table[:].indirect(two_t[:]))
+
+        w2_grouped = keep.tile([P, PACK * N], BF16, name="w2_grouped", align_bytes=64)
+        nc.gpsimd.tensor_scalar(
+            w2_grouped[:].rearrange("p (t m j) -> p m j t", t=PACK, j=PACK),
+            w2_raw[:].rearrange("p j (m t) -> p m j t", t=PACK),
+            1.0,
+            0.0,
+            ALU.mult,
+            ALU.add,
+        )
+        sums = keep.tile([P, PACK, N], F32, name="sums")
+        logs = keep.tile([P, PACK, N], F32, name="logs")
+        numer = keep.tile([P, PACK, N], F32, name="numer")
+        for t in range(PACK):
+            nc.scalar.activation(win_abs[t][:, :N], banks_a[t][:], ACT.Abs)
+        for t in range(PACK):
+            nc.vector.tensor_copy(win_a[t][:, N:], win_abs[t][:].indirect(n2_t[:]))
+            adder = nc.gpsimd if t < 3 else nc.vector
+            adder.tensor_tensor(sums[:, t, :], win_a[t][:, N:], win_abs[t][:, :N], ALU.add)
+            if t == 1:
+                quantize(w2q, w2_grouped, whole)
+        for t in range(PACK):
+            product(banks_b[t], w2q, t, xb, whole)
+        for t in range(PACK):
+            nc.scalar.activation(win_a[t][:, :N], banks_a[t][:], ACT.Copy, scale=ga_t[:, t : t + 1])
+        for t in range(PACK):
+            nc.scalar.activation(logs[:, t, :], sums[:, t, :], ACT.Ln, bias=1.0, scale=4.0)
+            if t < PACK - 1:
+                nc.scalar.copy(win_b[t][:, :N], banks_b[t][:])
+        for t in range(PACK):
+            nc.vector.tensor_copy(numer[:, t, :], win_a[t][:].indirect(n1_t[:]))
+
+        z_planes = keep.tile([P, PACK, N], BF16, name="z_planes")
+        z2_planes = keep.tile([P, PACK, N], BF16, name="z2_planes")
+        for c in range(PACK):
+            cols = slice(c * P, (c + 1) * P)
+            recip = win_b[c][:, N:].rearrange("p (t n) -> p t n", t=PACK)
+            nc.scalar.activation(recip, logs[:, :, cols], ACT.Sigmoid, scale=-1.0)
+            nc.vector.scalar_tensor_tensor(z_planes[:, :, cols], numer[:, :, cols], 4.0, recip, ALU.mult, ALU.mult)
+        nc.scalar.copy(win_b[PACK - 1][:, :N], banks_b[PACK - 1][:])
+        z_grouped = keep.tile([P, PACK * N], BF16, name="z_grouped", align_bytes=64)
+        nc.vector.tensor_copy(
+            z_grouped[:].rearrange("p (u m t) -> p m t u", u=PACK, t=PACK),
+            z_planes[:].rearrange("p t (m u) -> p m t u", u=PACK),
+        )
+        zq = mx_tiles("zq")
+        z2q = mx_tiles("z2q")
+        quantize(zq, z_grouped, whole)
+        z2_grouped = keep.tile([P, PACK * N], BF16, name="z2_grouped", align_bytes=64)
+        banks_s = [psum.tile([P, N], F32, name="bank_s%d" % u, tag="first%d" % u) for u in range(PACK)]
+        for cols in halves:
+            entries = slice(cols.start // 16, cols.stop // 16)
+            for t in range(PACK):
+                nc.scalar.activation(sums[:, t, cols], win_b[t][:].indirect(n3_t[:, entries]), ACT.Sigmoid)
+                nc.vector.scalar_tensor_tensor(
+                    z2_planes[:, t, cols], banks_b[t][:, cols], gb_t[:, t : t + 1], sums[:, t, cols], ALU.mult, ALU.mult
+                )
+            nc.vector.tensor_copy(
+                z2_grouped[:, PACK * cols.start : PACK * cols.stop].rearrange("p (c i t) -> p c t i", i=4, t=PACK),
+                z2_planes[:, :, cols].rearrange("p t (c i) -> p c t i", i=4),
+            )
+            quantize(z2q, z2_grouped, cols)
+            for u in range(PACK):
+                product(banks_s[u], zq, u, z2q, cols)
+
+        out_rows = out.rearrange("(p u) v -> u p v", u=PACK)
+        for u in range(PACK):
+            nc.scalar.activation(win_abs[u][:, :N], banks_s[u][:], ACT.Copy, scale=0.125)
+        for u in range(PACK):
+            nc.vector.tensor_copy(logs[:, u, :], win_abs[u][:].indirect(n4_t[:]))
+            if u < 3:
+                nc.gpsimd.tensor_tensor(win_a[u][:, :N], logs[:, u, :], win_abs[u][:, :N], ALU.add)
+            else:
+                nc.vector.scalar_tensor_tensor(
+                    win_a[u][:, :N], banks_s[u][:], 0.125, logs[:, u, :], ALU.mult, ALU.add
+                )
+        for u in range(PACK):
+            for cols in [whole] if u < PACK - 1 else halves:
+                entries = slice(cols.start // 16, cols.stop // 16)
+                nc.scalar.activation(sums[:, u, cols], win_a[u][:].indirect(n5_t[:, entries]), ACT.Sigmoid)
+                nc.vector.scalar_tensor_tensor(
+                    numer[:, u, cols], sums[:, u, cols], 0.5, win_a[u][:, cols], ALU.subtract, ALU.mult
+                )
+                nc.sync.dma_start(out_rows[u][:, cols], numer[:, u, cols])

@@ -41,8 +41,9 @@ def tile_picked_kqnorm2gatehopp_none_p_kernel(
         nc.vector.memset(scale_table[:].bitcast(I32), 0)
 
         half = N // 2
-        word_table = keep.tile([P, T], U32, name="word_table", align_bytes=64)
-        nc.sync.dma_start(word_table[:].bitcast(I32), x_words[0].rearrange("p n t -> p (n t)").bitcast(I32))
+        w1_raw = [keep.tile([P, PACK, half], F32, name="w1_raw%d" % h) for h in range(2)]
+        w1_rows = w1.rearrange("(p j) c -> p j c", j=PACK)
+        nc.sync.dma_start(w1_raw[0][:], w1_rows[:, :, :half])
         for q in range(4):
             nc.sync.dma_start(
                 scale_table[32 * q : 32 * q + 4, :].bitcast(I32),
@@ -50,16 +51,15 @@ def tile_picked_kqnorm2gatehopp_none_p_kernel(
             )
         offs_t = load_list(offs, "offs_t")
         two_t = load_list(two, "two_t")
-        w1_raw = [keep.tile([P, PACK, half], F32, name="w1_raw%d" % h) for h in range(2)]
-        w1_rows = w1.rearrange("(p j) c -> p j c", j=PACK)
-        for h in range(2):
-            nc.sync.dma_start(w1_raw[h][:], w1_rows[:, :, h * half : (h + 1) * half])
+        nc.sync.dma_start(w1_raw[1][:], w1_rows[:, :, half:])
         n2_t = load_list(n2, "n2_t")
         ga_t = keep.tile([P, PACK], F32, name="ga_t")
         nc.sync.dma_start(ga_t[:], ga.rearrange("(p t) o -> p (t o)", t=PACK))
-        n1_t = load_list(n1, "n1_t")
+        word_table = keep.tile([P, T], U32, name="word_table", align_bytes=64)
+        nc.sync.dma_start(word_table[:].bitcast(I32), x_words[0].rearrange("p n t -> p (n t)").bitcast(I32))
         w2_raw = keep.tile([P, PACK, N], F32, name="w2_raw")
         nc.sync.dma_start(w2_raw[:], w2.rearrange("(p j) c -> p j c", j=PACK))
+        n1_t = load_list(n1, "n1_t")
         n3_t = load_list(n3, "n3_t")
         gb_t = keep.tile([P, PACK], F32, name="gb_t")
         nc.sync.dma_start(gb_t[:], gb.rearrange("(p t) o -> p (t o)", t=PACK))
@@ -98,15 +98,14 @@ def tile_picked_kqnorm2gatehopp_none_p_kernel(
 
         whole = slice(0, N)
         halves = [slice(0, half), slice(half, N)]
-        xa = mx_tiles("xa")
+        xa_scales = keep.tile([P, N], U8, name="xa_scales", align_bytes=64)
         xb = mx_tiles("xb")
         w1q = mx_tiles("w1q")
         w2q = mx_tiles("w2q")
-        nc.vector.tensor_copy(xa[0][:], word_table[:].indirect(offs_t[:]))
-        nc.vector.tensor_copy(xb[0][:], word_table[:].indirect(two_t[:]))
-        nc.vector.tensor_copy(xa[1][:], scale_table[:].indirect(offs_t[:]))
+        nc.vector.tensor_copy(xa_scales[:], scale_table[:].indirect(offs_t[:]))
+        nc.vector.tensor_copy(xb[1][:], scale_table[:].indirect(two_t[:]))
 
-        w1_grouped = keep.tile([P, PACK * N], BF16, name="w1_grouped", align_bytes=64)
+        w1_grouped = keep.tile([P, PACK * N], BF16, name="w1_grouped", tag="w1_stage", align_bytes=64)
         w1_view = w1_grouped[:].rearrange("p (t m j) -> p m j t", t=PACK, j=PACK)
         for h in range(2):
             nc.scalar.copy(
@@ -115,56 +114,57 @@ def tile_picked_kqnorm2gatehopp_none_p_kernel(
             )
         banks_a = [psum.tile([P, N], F32, name="bank_a%d" % t, tag="first%d" % t) for t in range(PACK)]
         banks_b = [psum.tile([P, N], F32, name="bank_b%d" % t) for t in range(PACK)]
-        for pair in halves:
-            quantize(w1q, w1_grouped, pair)
+        quantize(w1q, w1_grouped, whole)
+        xa_codes = keep.tile([P, N], U32, name="xa_codes", tag="w1_stage", align_bytes=64)
+        xa = (xa_codes, xa_scales)
+        nc.vector.tensor_copy(xa[0][:], word_table[:].indirect(offs_t[:]))
         for t in range(PACK):
             product(banks_a[t], w1q, t, xa, whole)
-        nc.vector.tensor_copy(xb[1][:], scale_table[:].indirect(two_t[:]))
+        nc.vector.tensor_copy(xb[0][:], word_table[:].indirect(two_t[:]))
+        ga4 = keep.tile([P, PACK], F32, name="ga4")
+        nc.vector.tensor_scalar(ga4[:], ga_t[:], 4.0, None, ALU.mult)
 
         w2_grouped = keep.tile([P, PACK * N], BF16, name="w2_grouped", align_bytes=64)
-        nc.gpsimd.tensor_scalar(
-            w2_grouped[:].rearrange("p (t m j) -> p m j t", t=PACK, j=PACK),
-            w2_raw[:].rearrange("p j (m t) -> p m j t", t=PACK),
-            1.0,
-            0.0,
-            ALU.mult,
-            ALU.add,
-        )
         sums = keep.tile([P, PACK, N], F32, name="sums")
         logs = keep.tile([P, PACK, N], F32, name="logs")
-        numer = keep.tile([P, PACK, N], F32, name="numer")
+        numer = w2_raw
         for t in range(PACK):
             nc.scalar.activation(win_abs[t][:, :N], banks_a[t][:], ACT.Abs)
         for t in range(PACK):
             nc.vector.tensor_copy(win_a[t][:, N:], win_abs[t][:].indirect(n2_t[:]))
-            adder = nc.gpsimd if t < 3 else nc.vector
+            adder = nc.gpsimd if t < 4 else nc.vector
             adder.tensor_tensor(sums[:, t, :], win_a[t][:, N:], win_abs[t][:, :N], ALU.add)
-            if t == 1:
+            if t == 0:
+                nc.vector.tensor_copy(
+                    w2_grouped[:].rearrange("p (t m j) -> p m j t", t=PACK, j=PACK),
+                    w2_raw[:].rearrange("p j (m t) -> p m j t", t=PACK),
+                )
+            if t == 0:
                 quantize(w2q, w2_grouped, whole)
         for t in range(PACK):
             product(banks_b[t], w2q, t, xb, whole)
         for t in range(PACK):
-            nc.scalar.activation(win_a[t][:, :N], banks_a[t][:], ACT.Copy, scale=ga_t[:, t : t + 1])
+            nc.scalar.activation(win_a[t][:, :N], banks_a[t][:], ACT.Copy, scale=ga4[:, t : t + 1])
+        for t in range(PACK):
+            nc.scalar.copy(win_b[t][:, :N], banks_b[t][:])
         for t in range(PACK):
             nc.scalar.activation(logs[:, t, :], sums[:, t, :], ACT.Ln, bias=1.0, scale=4.0)
-            if t < PACK - 1:
-                nc.scalar.copy(win_b[t][:, :N], banks_b[t][:])
         for t in range(PACK):
             nc.vector.tensor_copy(numer[:, t, :], win_a[t][:].indirect(n1_t[:]))
 
-        z_planes = keep.tile([P, PACK, N], BF16, name="z_planes")
-        z2_planes = keep.tile([P, PACK, N], BF16, name="z2_planes")
+        z_grouped = keep.tile([P, PACK * N], BF16, name="z_grouped", align_bytes=64)
+        z_view = z_grouped[:].rearrange("p (u m t) -> p m t u", u=PACK, t=PACK)
+        z2_planes = keep.tile([P, PACK, half], BF16, name="z2_planes")
         for c in range(PACK):
             cols = slice(c * P, (c + 1) * P)
             recip = win_b[c][:, N:].rearrange("p (t n) -> p t n", t=PACK)
             nc.scalar.activation(recip, logs[:, :, cols], ACT.Sigmoid, scale=-1.0)
-            nc.vector.scalar_tensor_tensor(z_planes[:, :, cols], numer[:, :, cols], 4.0, recip, ALU.mult, ALU.mult)
-        nc.scalar.copy(win_b[PACK - 1][:, :N], banks_b[PACK - 1][:])
-        z_grouped = keep.tile([P, PACK * N], BF16, name="z_grouped", align_bytes=64)
-        nc.vector.tensor_copy(
-            z_grouped[:].rearrange("p (u m t) -> p m t u", u=PACK, t=PACK),
-            z_planes[:].rearrange("p t (m u) -> p m t u", u=PACK),
-        )
+            nc.vector.tensor_tensor(
+                z_view[:, c * 32 : (c + 1) * 32, :, :],
+                numer[:, :, cols].rearrange("p t (m u) -> p m t u", u=PACK),
+                recip.rearrange("p t (m u) -> p m t u", u=PACK),
+                ALU.mult,
+            )
         zq = mx_tiles("zq")
         z2q = mx_tiles("z2q")
         quantize(zq, z_grouped, whole)
@@ -175,19 +175,19 @@ def tile_picked_kqnorm2gatehopp_none_p_kernel(
             for t in range(PACK):
                 nc.scalar.activation(sums[:, t, cols], win_b[t][:].indirect(n3_t[:, entries]), ACT.Sigmoid)
                 nc.vector.scalar_tensor_tensor(
-                    z2_planes[:, t, cols], banks_b[t][:, cols], gb_t[:, t : t + 1], sums[:, t, cols], ALU.mult, ALU.mult
+                    z2_planes[:, t, :], banks_b[t][:, cols], gb_t[:, t : t + 1], sums[:, t, cols], ALU.mult, ALU.mult
                 )
             nc.vector.tensor_copy(
                 z2_grouped[:, PACK * cols.start : PACK * cols.stop].rearrange("p (c i t) -> p c t i", i=4, t=PACK),
-                z2_planes[:, :, cols].rearrange("p t (c i) -> p c t i", i=4),
+                z2_planes[:].rearrange("p t (c i) -> p c t i", i=4),
             )
             quantize(z2q, z2_grouped, cols)
             for u in range(PACK):
                 product(banks_s[u], zq, u, z2q, cols)
+            for u in range(PACK):
+                nc.scalar.activation(win_abs[u][:, cols], banks_s[u][:, cols], ACT.Copy, scale=0.125)
 
         out_rows = out.rearrange("(p u) v -> u p v", u=PACK)
-        for u in range(PACK):
-            nc.scalar.activation(win_abs[u][:, :N], banks_s[u][:], ACT.Copy, scale=0.125)
         for u in range(PACK):
             nc.vector.tensor_copy(logs[:, u, :], win_abs[u][:].indirect(n4_t[:]))
             if u < 3:

@@ -1,6 +1,7 @@
 from contextlib import ExitStack
 
 import concourse.mybir as mybir
+from concourse.masks import make_identity
 
 F32 = mybir.dt.float32
 BF16 = mybir.dt.bfloat16
@@ -33,12 +34,13 @@ def tile_picked_kqnorm2gatehopp_none_p_kernel(
             nc.sync.dma_start(tile[:], src)
             return tile
 
+        scale_table = keep.tile([P, T], U8, name="scale_table", align_bytes=64)
+        nc.vector.memset(scale_table[:, : T // 2].bitcast(I32), 0)
+        nc.gpsimd.memset(scale_table[:, T // 2 :].bitcast(I32), 0)
         warm = keep.tile([P, 2], F32, name="warm")
         nc.vector.memset(warm[:, 0:1], 1.0)
         nc.scalar.activation(warm[:, 1:2], warm[:, 0:1], ACT.Ln)
 
-        scale_table = keep.tile([P, T], U8, name="scale_table", align_bytes=64)
-        nc.vector.memset(scale_table[:].bitcast(I32), 0)
 
         half = N // 2
         w1_raw = [keep.tile([P, PACK, half], F32, name="w1_raw%d" % h) for h in range(2)]
@@ -96,6 +98,9 @@ def tile_picked_kqnorm2gatehopp_none_p_kernel(
                 stop=True,
             )
 
+        identity = keep.tile([P, P], F32, name="identity")
+        make_identity(nc, identity[:])
+
         whole = slice(0, N)
         halves = [slice(0, half), slice(half, N)]
         xa_scales = keep.tile([P, N], U8, name="xa_scales", align_bytes=64)
@@ -132,8 +137,6 @@ def tile_picked_kqnorm2gatehopp_none_p_kernel(
             nc.scalar.activation(win_abs[t][:, :N], banks_a[t][:], ACT.Abs)
         for t in range(PACK):
             nc.vector.tensor_copy(win_a[t][:, N:], win_abs[t][:].indirect(n2_t[:]))
-            adder = nc.gpsimd if t < 4 else nc.vector
-            adder.tensor_tensor(sums[:, t, :], win_a[t][:, N:], win_abs[t][:, :N], ALU.add)
             if t == 0:
                 nc.vector.tensor_copy(
                     w2_grouped[:].rearrange("p (t m j) -> p m j t", t=PACK, j=PACK),
@@ -148,7 +151,18 @@ def tile_picked_kqnorm2gatehopp_none_p_kernel(
         for t in range(PACK):
             nc.scalar.copy(win_b[t][:, :N], banks_b[t][:])
         for t in range(PACK):
-            nc.scalar.activation(logs[:, t, :], sums[:, t, :], ACT.Ln, bias=1.0, scale=4.0)
+            bank = psum.tile([P, N], F32, name="bank_d%d" % t, tag="first%d" % t)
+            for c in range(PACK):
+                cols = slice(c * P, (c + 1) * P)
+                nc.tensor.matmul(bank[:, cols], win_abs[t][:, cols], identity[:], start=True, stop=False, is_transpose=True)
+                nc.tensor.matmul(
+                    bank[:, cols], win_a[t][:, N + c * P : N + (c + 1) * P], identity[:], start=False, stop=True, is_transpose=True
+                )
+            nc.scalar.activation(logs[:, t, :], bank[:], ACT.Ln, bias=1.0, scale=4.0)
+        banks_l = [psum.tile([P, PACK, P], F32, name="bank_l%d" % c, tag="first%d" % c) for c in range(PACK)]
+        for c in range(PACK):
+            for t in range(PACK):
+                nc.tensor.transpose(banks_l[c][:, t, :], logs[:, t, c * P : (c + 1) * P], identity[:])
         for t in range(PACK):
             nc.vector.tensor_copy(numer[:, t, :], win_a[t][:].indirect(n1_t[:]))
 
@@ -158,7 +172,7 @@ def tile_picked_kqnorm2gatehopp_none_p_kernel(
         for c in range(PACK):
             cols = slice(c * P, (c + 1) * P)
             recip = win_b[c][:, N:].rearrange("p (t n) -> p t n", t=PACK)
-            nc.scalar.activation(recip, logs[:, :, cols], ACT.Sigmoid, scale=-1.0)
+            nc.scalar.activation(recip, banks_l[c][:], ACT.Sigmoid, scale=-1.0)
             nc.vector.tensor_tensor(
                 z_view[:, c * 32 : (c + 1) * 32, :, :],
                 numer[:, :, cols].rearrange("p t (m u) -> p m t u", u=PACK),
@@ -189,13 +203,11 @@ def tile_picked_kqnorm2gatehopp_none_p_kernel(
 
         out_rows = out.rearrange("(p u) v -> u p v", u=PACK)
         for u in range(PACK):
-            nc.vector.tensor_copy(logs[:, u, :], win_abs[u][:].indirect(n4_t[:]))
-            if u < 3:
-                nc.gpsimd.tensor_tensor(win_a[u][:, :N], logs[:, u, :], win_abs[u][:, :N], ALU.add)
+            if u < 2:
+                nc.vector.tensor_copy(logs[:, u, :], win_abs[u][:, :N])
             else:
-                nc.vector.scalar_tensor_tensor(
-                    win_a[u][:, :N], banks_s[u][:], 0.125, logs[:, u, :], ALU.mult, ALU.add
-                )
+                nc.scalar.activation(logs[:, u, :], banks_s[u][:], ACT.Copy, scale=0.125)
+            nc.vector.tensor_tensor(win_a[u][:, :N], win_abs[u][:].indirect(n4_t[:]), logs[:, u, :], ALU.add)
         for u in range(PACK):
             for cols in [whole] if u < PACK - 1 else halves:
                 entries = slice(cols.start // 16, cols.stop // 16)

@@ -1,7 +1,6 @@
 from contextlib import ExitStack
 
 import concourse.mybir as mybir
-from concourse.masks import make_identity
 
 F32 = mybir.dt.float32
 BF16 = mybir.dt.bfloat16
@@ -15,8 +14,13 @@ ALU = mybir.AluOpType
 
 P = 128
 PACK = 4
-T = 2048
+TOKENS = 2048
 N = 512
+HALF = N // 2
+GROUP = 16
+QUADRANTS = 4
+S_SCALE = 2 * 0.0625
+COPIES_ON_VECTOR = 2
 FLOPS = 3 * 2 * 512 * 512 * 512
 
 
@@ -24,55 +28,17 @@ def tile_picked_kqnorm2gatehopp_none_p_kernel(
     tc, x_words, x_scales, w1, w2, ga, gb, offs, two, n1, n2, n3, n4, n5, out
 ):
     nc = tc.nc
+    whole = slice(0, N)
+    halves = [slice(0, HALF), slice(HALF, N)]
     with ExitStack() as ctx:
         lists = ctx.enter_context(tc.tile_pool(name="lists", bufs=1))
         keep = ctx.enter_context(tc.tile_pool(name="keep", bufs=1))
         psum = ctx.enter_context(tc.psum_pool(name="psum", bufs=1))
 
         def load_list(src, name):
-            tile = lists.tile([P, N // 16], U16, name=name)
+            tile = lists.tile([P, N // GROUP], U16, name=name)
             nc.sync.dma_start(tile[:], src)
             return tile
-
-        scale_table = keep.tile([P, T], U8, name="scale_table", align_bytes=64)
-        nc.vector.memset(scale_table[:, : T // 2].bitcast(I32), 0)
-        nc.gpsimd.memset(scale_table[:, T // 2 :].bitcast(I32), 0)
-        warm = keep.tile([P, 2], F32, name="warm")
-        nc.vector.memset(warm[:, 0:1], 1.0)
-        nc.scalar.activation(warm[:, 1:2], warm[:, 0:1], ACT.Ln)
-
-
-        half = N // 2
-        w1_raw = [keep.tile([P, PACK, half], F32, name="w1_raw%d" % h) for h in range(2)]
-        w1_rows = w1.rearrange("(p j) c -> p j c", j=PACK)
-        nc.sync.dma_start(w1_raw[0][:], w1_rows[:, :, :half])
-        for q in range(4):
-            nc.sync.dma_start(
-                scale_table[32 * q : 32 * q + 4, :].bitcast(I32),
-                x_scales[0, 4 * q : 4 * q + 4, :].bitcast(I32),
-            )
-        offs_t = load_list(offs, "offs_t")
-        two_t = load_list(two, "two_t")
-        nc.sync.dma_start(w1_raw[1][:], w1_rows[:, :, half:])
-        n2_t = load_list(n2, "n2_t")
-        ga_t = keep.tile([P, PACK], F32, name="ga_t")
-        nc.sync.dma_start(ga_t[:], ga.rearrange("(p t) o -> p (t o)", t=PACK))
-        word_table = keep.tile([P, T], U32, name="word_table", align_bytes=64)
-        nc.sync.dma_start(word_table[:].bitcast(I32), x_words[0].rearrange("p n t -> p (n t)").bitcast(I32))
-        w2_raw = keep.tile([P, PACK, N], F32, name="w2_raw")
-        nc.sync.dma_start(w2_raw[:], w2.rearrange("(p j) c -> p j c", j=PACK))
-        n1_t = load_list(n1, "n1_t")
-        n3_t = load_list(n3, "n3_t")
-        gb_t = keep.tile([P, PACK], F32, name="gb_t")
-        nc.sync.dma_start(gb_t[:], gb.rearrange("(p t) o -> p (t o)", t=PACK))
-        n4_t = load_list(n4, "n4_t")
-        n5_t = load_list(n5, "n5_t")
-
-        win_abs = [keep.tile([P, 2 * N], F32, name="win_abs%d" % t) for t in range(PACK)]
-        win_a = [keep.tile([P, 2 * N], F32, name="win_a%d" % t) for t in range(PACK)]
-        win_b = [keep.tile([P, 2 * N], F32, name="win_b%d" % t) for t in range(PACK)]
-        for t in range(PACK):
-            nc.vector.memset(win_abs[t][:, N:], 0.0)
 
         def mx_tiles(name):
             codes = keep.tile([P, N], U32, name=name + "_codes", align_bytes=64)
@@ -86,8 +52,8 @@ def tile_picked_kqnorm2gatehopp_none_p_kernel(
                 in_=grouped[:, PACK * cols.start : PACK * cols.stop],
             )
 
-        def product(bank, lhs, t, rhs, cols):
-            rows = slice(t * P, (t + 1) * P)
+        def product(bank, lhs, plane, rhs, cols):
+            rows = slice(plane * P, (plane + 1) * P)
             nc.tensor.matmul_mx(
                 out=bank[:, cols],
                 lhsT=lhs[0][:, rows].bitcast(FP8X4),
@@ -98,98 +64,123 @@ def tile_picked_kqnorm2gatehopp_none_p_kernel(
                 stop=True,
             )
 
-        identity = keep.tile([P, P], F32, name="identity")
-        make_identity(nc, identity[:])
+        def entries(cols):
+            return slice(cols.start // GROUP, cols.stop // GROUP)
 
-        whole = slice(0, N)
-        halves = [slice(0, half), slice(half, N)]
-        xa_scales = keep.tile([P, N], U8, name="xa_scales", align_bytes=64)
+        scale_table = keep.tile([P, TOKENS], U8, name="scale_table", align_bytes=64)
+        nc.vector.memset(scale_table[:].bitcast(I32), 0)
+
+        one_zero = keep.tile([P, 2], F32, name="one_zero")
+        nc.vector.memset(one_zero[:, 0:1], 1.0)
+        nc.scalar.activation(one_zero[:, 1:2], one_zero[:, 0:1], ACT.Ln)
+        zero = one_zero[:, 1:2]
+
+        w1_raw = [keep.tile([P, PACK, HALF], F32, name="w1_raw%d" % h) for h in range(2)]
+        w1_rows = w1.rearrange("(p j) c -> p j c", j=PACK)
+        word_table = keep.tile([P, TOKENS], U32, name="word_table", align_bytes=64)
+        nc.sync.dma_start(word_table[:].bitcast(I32), x_words[0].rearrange("p n t -> p (n t)").bitcast(I32))
+        offs_t = load_list(offs, "offs_t")
+        for q in range(QUADRANTS):
+            nc.sync.dma_start(
+                scale_table[32 * q : 32 * q + 4, :].bitcast(I32),
+                x_scales[0, 4 * q : 4 * q + 4, :].bitcast(I32),
+            )
+        two_t = load_list(two, "two_t")
+        for h in range(2):
+            nc.sync.dma_start(w1_raw[h][:], w1_rows[:, :, halves[h]])
+        n2_t = load_list(n2, "n2_t")
+        ga_t = keep.tile([P, PACK], F32, name="ga_t")
+        nc.sync.dma_start(ga_t[:], ga.rearrange("(p t) o -> p (t o)", t=PACK))
+        w2_raw = keep.tile([P, PACK, N], F32, name="w2_raw", tag="w2_stage")
+        nc.sync.dma_start(w2_raw[:], w2.rearrange("(p j) c -> p j c", j=PACK))
+        n1_t = load_list(n1, "n1_t")
+        n3_t = load_list(n3, "n3_t")
+        gb_t = keep.tile([P, PACK], F32, name="gb_t")
+        nc.sync.dma_start(gb_t[:], gb.rearrange("(p t) o -> p (t o)", t=PACK))
+        n4_t = load_list(n4, "n4_t")
+        n5_t = load_list(n5, "n5_t")
+
+        first = [keep.tile([P, 2 * N], F32, name="first%d" % t) for t in range(PACK)]
+        second = [keep.tile([P, 2 * N], F32, name="second%d" % t) for t in range(PACK)]
+        third = [keep.tile([P, 2 * N], F32, name="third%d" % t) for t in range(PACK)]
+        for t in range(PACK):
+            nc.vector.memset(first[t][:, N:], 0.0)
+
+        xa = mx_tiles("xa")
         xb = mx_tiles("xb")
         w1q = mx_tiles("w1q")
         w2q = mx_tiles("w2q")
-        nc.vector.tensor_copy(xa_scales[:], scale_table[:].indirect(offs_t[:]))
+        nc.vector.tensor_copy(xa[0][:], word_table[:].indirect(offs_t[:]))
+        nc.vector.tensor_copy(xa[1][:], scale_table[:].indirect(offs_t[:]))
+        nc.vector.tensor_copy(xb[0][:], word_table[:].indirect(two_t[:]))
         nc.vector.tensor_copy(xb[1][:], scale_table[:].indirect(two_t[:]))
 
-        w1_grouped = keep.tile([P, PACK * N], BF16, name="w1_grouped", tag="w1_stage", align_bytes=64)
-        w1_view = w1_grouped[:].rearrange("p (t m j) -> p m j t", t=PACK, j=PACK)
+        w1_grouped = keep.tile([P, PACK * N], BF16, name="w1_grouped", align_bytes=64)
+        w1_dealt = w1_grouped[:].rearrange("p (t m j) -> p m j t", t=PACK, j=PACK)
         for h in range(2):
             nc.scalar.copy(
-                w1_view[:, h * (P // 2) : (h + 1) * (P // 2), :, :],
+                w1_dealt[:, h * (P // 2) : (h + 1) * (P // 2), :, :],
                 w1_raw[h][:].rearrange("p j (m t) -> p m j t", t=PACK),
             )
-        banks_a = [psum.tile([P, N], F32, name="bank_a%d" % t, tag="first%d" % t) for t in range(PACK)]
-        banks_b = [psum.tile([P, N], F32, name="bank_b%d" % t) for t in range(PACK)]
+        banks_a = [psum.tile([P, N], F32, name="bank_a%d" % t, tag="a_then_s%d" % t) for t in range(PACK)]
         quantize(w1q, w1_grouped, whole)
-        xa_codes = keep.tile([P, N], U32, name="xa_codes", tag="w1_stage", align_bytes=64)
-        xa = (xa_codes, xa_scales)
-        nc.vector.tensor_copy(xa[0][:], word_table[:].indirect(offs_t[:]))
         for t in range(PACK):
             product(banks_a[t], w1q, t, xa, whole)
-        nc.vector.tensor_copy(xb[0][:], word_table[:].indirect(two_t[:]))
         ga4 = keep.tile([P, PACK], F32, name="ga4")
         nc.vector.tensor_scalar(ga4[:], ga_t[:], 4.0, None, ALU.mult)
 
         w2_grouped = keep.tile([P, PACK * N], BF16, name="w2_grouped", align_bytes=64)
-        sums = keep.tile([P, PACK, N], F32, name="sums")
-        logs = keep.tile([P, PACK, N], F32, name="logs")
-        numer = w2_raw
-        for t in range(PACK):
-            nc.scalar.activation(win_abs[t][:, :N], banks_a[t][:], ACT.Abs)
-        for t in range(PACK):
-            nc.vector.tensor_copy(win_a[t][:, N:], win_abs[t][:].indirect(n2_t[:]))
-            if t == 0:
-                nc.vector.tensor_copy(
-                    w2_grouped[:].rearrange("p (t m j) -> p m j t", t=PACK, j=PACK),
-                    w2_raw[:].rearrange("p j (m t) -> p m j t", t=PACK),
-                )
-            if t == 0:
-                quantize(w2q, w2_grouped, whole)
+        nc.vector.tensor_copy(
+            w2_grouped[:].rearrange("p (t m j) -> p m j t", t=PACK, j=PACK),
+            w2_raw[:].rearrange("p j (m t) -> p m j t", t=PACK),
+        )
+        quantize(w2q, w2_grouped, whole)
+        banks_b = [psum.tile([P, N], F32, name="bank_b%d" % t) for t in range(PACK)]
         for t in range(PACK):
             product(banks_b[t], w2q, t, xb, whole)
+
+        stage_x = keep.tile([P, PACK, N], F32, name="stage_x", tag="w2_stage")
+        stage_y = keep.tile([P, PACK, N], F32, name="stage_y")
+        stage_z = keep.tile([P, PACK, N], F32, name="stage_z")
+
         for t in range(PACK):
-            nc.scalar.activation(win_a[t][:, :N], banks_a[t][:], ACT.Copy, scale=ga4[:, t : t + 1])
+            nc.scalar.activation(first[t][:, :N], banks_a[t][:], ACT.Abs, bias=zero)
         for t in range(PACK):
-            nc.scalar.copy(win_b[t][:, :N], banks_b[t][:])
+            nc.vector.tensor_copy(stage_x[:, t, :], first[t][:, :N])
+            nc.vector.tensor_tensor(second[t][:, N:], first[t][:].indirect(n2_t[:]), stage_x[:, t, :], ALU.add)
         for t in range(PACK):
-            bank = psum.tile([P, N], F32, name="bank_d%d" % t, tag="first%d" % t)
-            for c in range(PACK):
-                cols = slice(c * P, (c + 1) * P)
-                nc.tensor.matmul(bank[:, cols], win_abs[t][:, cols], identity[:], start=True, stop=False, is_transpose=True)
-                nc.tensor.matmul(
-                    bank[:, cols], win_a[t][:, N + c * P : N + (c + 1) * P], identity[:], start=False, stop=True, is_transpose=True
-                )
-            nc.scalar.activation(logs[:, t, :], bank[:], ACT.Ln, bias=1.0, scale=4.0)
-        banks_l = [psum.tile([P, PACK, P], F32, name="bank_l%d" % c, tag="first%d" % c) for c in range(PACK)]
-        for c in range(PACK):
-            for t in range(PACK):
-                nc.tensor.transpose(banks_l[c][:, t, :], logs[:, t, c * P : (c + 1) * P], identity[:])
+            nc.scalar.activation(second[t][:, :N], banks_a[t][:], ACT.Copy, scale=ga4[:, t : t + 1])
         for t in range(PACK):
-            nc.vector.tensor_copy(numer[:, t, :], win_a[t][:].indirect(n1_t[:]))
+            nc.scalar.copy(third[t][:, :N], banks_b[t][:])
+        for t in range(PACK):
+            nc.scalar.activation(stage_y[:, t, :], second[t][:, N:], ACT.Ln, bias=1.0, scale=4.0)
+        for t in range(PACK):
+            nc.vector.tensor_copy(stage_z[:, t, :], second[t][:].indirect(n1_t[:]))
 
         z_grouped = keep.tile([P, PACK * N], BF16, name="z_grouped", align_bytes=64)
-        z_view = z_grouped[:].rearrange("p (u m t) -> p m t u", u=PACK, t=PACK)
-        z2_planes = keep.tile([P, PACK, half], BF16, name="z2_planes")
+        z_dealt = z_grouped[:].rearrange("p (u m t) -> p m t u", u=PACK, t=PACK)
+        z2_planes = keep.tile([P, PACK, HALF], BF16, name="z2_planes")
         for c in range(PACK):
             cols = slice(c * P, (c + 1) * P)
-            recip = win_b[c][:, N:].rearrange("p (t n) -> p t n", t=PACK)
-            nc.scalar.activation(recip, banks_l[c][:], ACT.Sigmoid, scale=-1.0)
+            recip = third[c][:, N:].rearrange("p (t n) -> p t n", t=PACK)
+            nc.scalar.activation(recip, stage_y[:, :, cols], ACT.Sigmoid, scale=-1.0)
             nc.vector.tensor_tensor(
-                z_view[:, c * 32 : (c + 1) * 32, :, :],
-                numer[:, :, cols].rearrange("p t (m u) -> p m t u", u=PACK),
+                z_dealt[:, cols.start // PACK : cols.stop // PACK, :, :],
+                stage_z[:, :, cols].rearrange("p t (m u) -> p m t u", u=PACK),
                 recip.rearrange("p t (m u) -> p m t u", u=PACK),
                 ALU.mult,
             )
         zq = mx_tiles("zq")
         z2q = mx_tiles("z2q")
         quantize(zq, z_grouped, whole)
+
         z2_grouped = keep.tile([P, PACK * N], BF16, name="z2_grouped", align_bytes=64)
-        banks_s = [psum.tile([P, N], F32, name="bank_s%d" % u, tag="first%d" % u) for u in range(PACK)]
+        banks_s = [psum.tile([P, N], F32, name="bank_s%d" % u, tag="a_then_s%d" % u) for u in range(PACK)]
         for cols in halves:
-            entries = slice(cols.start // 16, cols.stop // 16)
             for t in range(PACK):
-                nc.scalar.activation(sums[:, t, cols], win_b[t][:].indirect(n3_t[:, entries]), ACT.Sigmoid)
+                nc.scalar.activation(stage_x[:, t, cols], third[t][:].indirect(n3_t[:, entries(cols)]), ACT.Sigmoid)
                 nc.vector.scalar_tensor_tensor(
-                    z2_planes[:, t, :], banks_b[t][:, cols], gb_t[:, t : t + 1], sums[:, t, cols], ALU.mult, ALU.mult
+                    z2_planes[:, t, :], banks_b[t][:, cols], gb_t[:, t : t + 1], stage_x[:, t, cols], ALU.mult, ALU.mult
                 )
             nc.vector.tensor_copy(
                 z2_grouped[:, PACK * cols.start : PACK * cols.stop].rearrange("p (c i t) -> p c t i", i=4, t=PACK),
@@ -199,20 +190,19 @@ def tile_picked_kqnorm2gatehopp_none_p_kernel(
             for u in range(PACK):
                 product(banks_s[u], zq, u, z2q, cols)
             for u in range(PACK):
-                nc.scalar.activation(win_abs[u][:, cols], banks_s[u][:, cols], ACT.Copy, scale=0.125)
+                nc.scalar.activation(first[u][:, cols], banks_s[u][:, cols], ACT.Copy, scale=S_SCALE)
 
         out_rows = out.rearrange("(p u) v -> u p v", u=PACK)
         for u in range(PACK):
-            if u < 2:
-                nc.vector.tensor_copy(logs[:, u, :], win_abs[u][:, :N])
+            if u < COPIES_ON_VECTOR:
+                nc.vector.tensor_copy(stage_y[:, u, :], first[u][:, :N])
             else:
-                nc.scalar.activation(logs[:, u, :], banks_s[u][:], ACT.Copy, scale=0.125)
-            nc.vector.tensor_tensor(win_a[u][:, :N], win_abs[u][:].indirect(n4_t[:]), logs[:, u, :], ALU.add)
+                nc.scalar.activation(stage_y[:, u, :], banks_s[u][:], ACT.Copy, scale=S_SCALE)
+            nc.vector.tensor_tensor(second[u][:, :N], first[u][:].indirect(n4_t[:]), stage_y[:, u, :], ALU.add)
         for u in range(PACK):
             for cols in [whole] if u < PACK - 1 else halves:
-                entries = slice(cols.start // 16, cols.stop // 16)
-                nc.scalar.activation(sums[:, u, cols], win_a[u][:].indirect(n5_t[:, entries]), ACT.Sigmoid)
+                nc.scalar.activation(stage_x[:, u, cols], second[u][:].indirect(n5_t[:, entries(cols)]), ACT.Sigmoid)
                 nc.vector.scalar_tensor_tensor(
-                    numer[:, u, cols], sums[:, u, cols], 0.5, win_a[u][:, cols], ALU.subtract, ALU.mult
+                    stage_z[:, u, cols], stage_x[:, u, cols], 0.5, second[u][:, cols], ALU.subtract, ALU.mult
                 )
-                nc.sync.dma_start(out_rows[u][:, cols], numer[:, u, cols])
+                nc.sync.dma_start(out_rows[u][:, cols], stage_z[:, u, cols])

@@ -20,7 +20,6 @@ HALF = N // 2
 GROUP = 16
 QUADRANTS = 4
 S_SCALE = 2 * 0.0625
-COPIES_ON_VECTOR = 2
 FLOPS = 3 * 2 * 512 * 512 * 512
 
 
@@ -123,7 +122,8 @@ def tile_picked_kqnorm2gatehopp_none_p_kernel(
                 w1_raw[h][:].rearrange("p j (m t) -> p m j t", t=PACK),
             )
         banks_a = [psum.tile([P, N], F32, name="bank_a%d" % t, tag="a_then_s%d" % t) for t in range(PACK)]
-        quantize(w1q, w1_grouped, whole)
+        for cols in (slice(0, P), slice(P, HALF), halves[1]):
+            quantize(w1q, w1_grouped, cols)
         for t in range(PACK):
             product(banks_a[t], w1q, t, xa, whole)
         ga4 = keep.tile([P, PACK], F32, name="ga4")
@@ -146,8 +146,8 @@ def tile_picked_kqnorm2gatehopp_none_p_kernel(
         for t in range(PACK):
             nc.scalar.activation(first[t][:, :N], banks_a[t][:], ACT.Abs, bias=zero)
         for t in range(PACK):
-            nc.vector.tensor_copy(stage_x[:, t, :], first[t][:, :N])
-            nc.vector.tensor_tensor(second[t][:, N:], first[t][:].indirect(n2_t[:]), stage_x[:, t, :], ALU.add)
+            nc.vector.tensor_copy(stage_x[:, t, :], first[t][:].indirect(n2_t[:]))
+            nc.gpsimd.tensor_tensor(second[t][:, N:], stage_x[:, t, :], first[t][:, :N], ALU.add)
         for t in range(PACK):
             nc.scalar.activation(second[t][:, :N], banks_a[t][:], ACT.Copy, scale=ga4[:, t : t + 1])
         for t in range(PACK):
@@ -191,13 +191,12 @@ def tile_picked_kqnorm2gatehopp_none_p_kernel(
                 product(banks_s[u], zq, u, z2q, cols)
             for u in range(PACK):
                 nc.scalar.activation(first[u][:, cols], banks_s[u][:, cols], ACT.Copy, scale=S_SCALE)
+                if u > 0:
+                    nc.scalar.activation(stage_y[:, u, cols], banks_s[u][:, cols], ACT.Copy, scale=S_SCALE)
 
         out_rows = out.rearrange("(p u) v -> u p v", u=PACK)
+        nc.vector.tensor_copy(stage_y[:, 0, :], first[0][:, :N])
         for u in range(PACK):
-            if u < COPIES_ON_VECTOR:
-                nc.vector.tensor_copy(stage_y[:, u, :], first[u][:, :N])
-            else:
-                nc.scalar.activation(stage_y[:, u, :], banks_s[u][:], ACT.Copy, scale=S_SCALE)
             nc.vector.tensor_tensor(second[u][:, :N], first[u][:].indirect(n4_t[:]), stage_y[:, u, :], ALU.add)
         for u in range(PACK):
             for cols in [whole] if u < PACK - 1 else halves:

from contextlib import ExitStack

import concourse.mybir as mybir

F32 = mybir.dt.float32
BF16 = mybir.dt.bfloat16
I32 = mybir.dt.int32
U32 = mybir.dt.uint32
U16 = mybir.dt.uint16
U8 = mybir.dt.uint8
FP8X4 = mybir.dt.float8_e4m3fn_x4
ACT = mybir.ActivationFunctionType
ALU = mybir.AluOpType

P = 128
PACK = 4
TOKENS = 2048
N = 512
HALF = N // 2
GROUP = 16
QUADRANTS = 4
S_SCALE = 2 * 0.0625
FLOPS = 3 * 2 * 512 * 512 * 512


def tile_picked_kqnorm2gatehopp_none_p_kernel(
    tc, x_words, x_scales, w1, w2, ga, gb, offs, two, n1, n2, n3, n4, n5, out
):
    nc = tc.nc
    whole = slice(0, N)
    halves = [slice(0, HALF), slice(HALF, N)]
    with ExitStack() as ctx:
        lists = ctx.enter_context(tc.tile_pool(name="lists", bufs=1))
        keep = ctx.enter_context(tc.tile_pool(name="keep", bufs=1))
        psum = ctx.enter_context(tc.psum_pool(name="psum", bufs=1))

        def load_list(src, name):
            tile = lists.tile([P, N // GROUP], U16, name=name)
            nc.sync.dma_start(tile[:], src)
            return tile

        def mx_tiles(name):
            codes = keep.tile([P, N], U32, name=name + "_codes", align_bytes=64)
            scales = keep.tile([P, N], U8, name=name + "_scales", align_bytes=64)
            return codes, scales

        def quantize(dst, grouped, cols):
            nc.vector.quantize_mx(
                out=dst[0][:, cols].bitcast(FP8X4),
                scales=dst[1][:, cols],
                in_=grouped[:, PACK * cols.start : PACK * cols.stop],
            )

        def product(bank, lhs, plane, rhs, cols):
            rows = slice(plane * P, (plane + 1) * P)
            nc.tensor.matmul_mx(
                out=bank[:, cols],
                lhsT=lhs[0][:, rows].bitcast(FP8X4),
                lhsT_scale=lhs[1][:, rows],
                rhs=rhs[0][:, cols].bitcast(FP8X4),
                rhs_scale=rhs[1][:, cols],
                start=True,
                stop=True,
            )

        def entries(cols):
            return slice(cols.start // GROUP, cols.stop // GROUP)

        scale_table = keep.tile([P, TOKENS], U8, name="scale_table", align_bytes=64)
        nc.vector.memset(scale_table[:].bitcast(I32), 0)

        one_zero = keep.tile([P, 2], F32, name="one_zero")
        nc.vector.memset(one_zero[:, 0:1], 1.0)
        nc.scalar.activation(one_zero[:, 1:2], one_zero[:, 0:1], ACT.Ln)
        zero = one_zero[:, 1:2]

        w1_raw = [keep.tile([P, PACK, HALF], F32, name="w1_raw%d" % h) for h in range(2)]
        w1_rows = w1.rearrange("(p j) c -> p j c", j=PACK)
        word_table = keep.tile([P, TOKENS], U32, name="word_table", align_bytes=64)
        nc.sync.dma_start(word_table[:].bitcast(I32), x_words[0].rearrange("p n t -> p (n t)").bitcast(I32))
        offs_t = load_list(offs, "offs_t")
        for q in range(QUADRANTS):
            nc.sync.dma_start(
                scale_table[32 * q : 32 * q + 4, :].bitcast(I32),
                x_scales[0, 4 * q : 4 * q + 4, :].bitcast(I32),
            )
        two_t = load_list(two, "two_t")
        for h in range(2):
            nc.sync.dma_start(w1_raw[h][:], w1_rows[:, :, halves[h]])
        n2_t = load_list(n2, "n2_t")
        ga_t = keep.tile([P, PACK], F32, name="ga_t")
        nc.sync.dma_start(ga_t[:], ga.rearrange("(p t) o -> p (t o)", t=PACK))
        w2_raw = keep.tile([P, PACK, N], F32, name="w2_raw", tag="w2_stage")
        nc.sync.dma_start(w2_raw[:], w2.rearrange("(p j) c -> p j c", j=PACK))
        n1_t = load_list(n1, "n1_t")
        n3_t = load_list(n3, "n3_t")
        gb_t = keep.tile([P, PACK], F32, name="gb_t")
        nc.sync.dma_start(gb_t[:], gb.rearrange("(p t) o -> p (t o)", t=PACK))
        n4_t = load_list(n4, "n4_t")
        n5_t = load_list(n5, "n5_t")

        first = [keep.tile([P, 2 * N], F32, name="first%d" % t) for t in range(PACK)]
        second = [keep.tile([P, 2 * N], F32, name="second%d" % t) for t in range(PACK)]
        third = [keep.tile([P, 2 * N], F32, name="third%d" % t) for t in range(PACK)]
        for t in range(PACK):
            nc.vector.memset(first[t][:, N:], 0.0)

        xa = mx_tiles("xa")
        xb = mx_tiles("xb")
        w1q = mx_tiles("w1q")
        w2q = mx_tiles("w2q")
        nc.vector.tensor_copy(xa[0][:], word_table[:].indirect(offs_t[:]))
        nc.vector.tensor_copy(xa[1][:], scale_table[:].indirect(offs_t[:]))
        nc.vector.tensor_copy(xb[0][:], word_table[:].indirect(two_t[:]))
        nc.vector.tensor_copy(xb[1][:], scale_table[:].indirect(two_t[:]))

        w1_grouped = keep.tile([P, PACK * N], BF16, name="w1_grouped", align_bytes=64)
        w1_dealt = w1_grouped[:].rearrange("p (t m j) -> p m j t", t=PACK, j=PACK)
        for h in range(2):
            nc.scalar.copy(
                w1_dealt[:, h * (P // 2) : (h + 1) * (P // 2), :, :],
                w1_raw[h][:].rearrange("p j (m t) -> p m j t", t=PACK),
            )
        banks_a = [psum.tile([P, N], F32, name="bank_a%d" % t, tag="a_then_s%d" % t) for t in range(PACK)]
        for cols in (slice(0, P), slice(P, HALF), halves[1]):
            quantize(w1q, w1_grouped, cols)
        for t in range(PACK):
            product(banks_a[t], w1q, t, xa, whole)
        ga4 = keep.tile([P, PACK], F32, name="ga4")
        nc.vector.tensor_scalar(ga4[:], ga_t[:], 4.0, None, ALU.mult)

        w2_grouped = keep.tile([P, PACK * N], BF16, name="w2_grouped", align_bytes=64)
        nc.vector.tensor_copy(
            w2_grouped[:].rearrange("p (t m j) -> p m j t", t=PACK, j=PACK),
            w2_raw[:].rearrange("p j (m t) -> p m j t", t=PACK),
        )
        quantize(w2q, w2_grouped, whole)
        banks_b = [psum.tile([P, N], F32, name="bank_b%d" % t) for t in range(PACK)]
        for t in range(PACK):
            product(banks_b[t], w2q, t, xb, whole)

        stage_x = keep.tile([P, PACK, N], F32, name="stage_x", tag="w2_stage")
        stage_y = keep.tile([P, PACK, N], F32, name="stage_y")
        stage_z = keep.tile([P, PACK, N], F32, name="stage_z")

        for t in range(PACK):
            nc.scalar.activation(first[t][:, :N], banks_a[t][:], ACT.Abs, bias=zero)
        for t in range(PACK):
            nc.vector.tensor_copy(stage_x[:, t, :], first[t][:].indirect(n2_t[:]))
            nc.gpsimd.tensor_tensor(second[t][:, N:], stage_x[:, t, :], first[t][:, :N], ALU.add)
        for t in range(PACK):
            nc.scalar.activation(second[t][:, :N], banks_a[t][:], ACT.Copy, scale=ga4[:, t : t + 1])
        for t in range(PACK):
            nc.scalar.copy(third[t][:, :N], banks_b[t][:])
        for t in range(PACK):
            nc.scalar.activation(stage_y[:, t, :], second[t][:, N:], ACT.Ln, bias=1.0, scale=4.0)
        for t in range(PACK):
            nc.vector.tensor_copy(stage_z[:, t, :], second[t][:].indirect(n1_t[:]))

        z_grouped = keep.tile([P, PACK * N], BF16, name="z_grouped", align_bytes=64)
        z_dealt = z_grouped[:].rearrange("p (u m t) -> p m t u", u=PACK, t=PACK)
        z2_planes = keep.tile([P, PACK, HALF], BF16, name="z2_planes")
        for c in range(PACK):
            cols = slice(c * P, (c + 1) * P)
            recip = third[c][:, N:].rearrange("p (t n) -> p t n", t=PACK)
            nc.scalar.activation(recip, stage_y[:, :, cols], ACT.Sigmoid, scale=-1.0)
            nc.vector.tensor_tensor(
                z_dealt[:, cols.start // PACK : cols.stop // PACK, :, :],
                stage_z[:, :, cols].rearrange("p t (m u) -> p m t u", u=PACK),
                recip.rearrange("p t (m u) -> p m t u", u=PACK),
                ALU.mult,
            )
        zq = mx_tiles("zq")
        z2q = mx_tiles("z2q")
        quantize(zq, z_grouped, whole)

        z2_grouped = keep.tile([P, PACK * N], BF16, name="z2_grouped", align_bytes=64)
        banks_s = [psum.tile([P, N], F32, name="bank_s%d" % u, tag="a_then_s%d" % u) for u in range(PACK)]
        for cols in halves:
            for t in range(PACK):
                nc.scalar.activation(stage_x[:, t, cols], third[t][:].indirect(n3_t[:, entries(cols)]), ACT.Sigmoid)
                nc.vector.scalar_tensor_tensor(
                    z2_planes[:, t, :], banks_b[t][:, cols], gb_t[:, t : t + 1], stage_x[:, t, cols], ALU.mult, ALU.mult
                )
            nc.vector.tensor_copy(
                z2_grouped[:, PACK * cols.start : PACK * cols.stop].rearrange("p (c i t) -> p c t i", i=4, t=PACK),
                z2_planes[:].rearrange("p t (c i) -> p c t i", i=4),
            )
            quantize(z2q, z2_grouped, cols)
            for u in range(PACK):
                product(banks_s[u], zq, u, z2q, cols)
            for u in range(PACK):
                nc.scalar.activation(first[u][:, cols], banks_s[u][:, cols], ACT.Copy, scale=S_SCALE)
                if u > 0:
                    nc.scalar.activation(stage_y[:, u, cols], banks_s[u][:, cols], ACT.Copy, scale=S_SCALE)

        out_rows = out.rearrange("(p u) v -> u p v", u=PACK)
        nc.vector.tensor_copy(stage_y[:, 0, :], first[0][:, :N])
        for u in range(PACK):
            nc.vector.tensor_tensor(second[u][:, :N], first[u][:].indirect(n4_t[:]), stage_y[:, u, :], ALU.add)
        for u in range(PACK):
            for cols in [whole] if u < PACK - 1 else halves:
                nc.scalar.activation(stage_x[:, u, cols], second[u][:].indirect(n5_t[:, entries(cols)]), ACT.Sigmoid)
                nc.vector.scalar_tensor_tensor(
                    stage_z[:, u, cols], stage_x[:, u, cols], 0.5, second[u][:, cols], ALU.subtract, ALU.mult
                )
                nc.sync.dma_start(out_rows[u][:, cols], stage_z[:, u, cols])
